import numpy as np, ml_dtypes
CORES = [36,164,52,180,100,228,116,244]
N = 8
BF = ml_dtypes.bfloat16
V, HB, CH, LV, RO = 1792, 1024, 96, 2, 4
def places(w, dd):
    u = np.matmul(np.swapaxes(w, -1, -2), dd) & 4095
    return (((u * u) >> 5) + u) & (HB - 1)
def pattern(rng):
    return np.stack([np.tile(rng.integers(0, 256, a), 16 // a) for a in (int(v) for v in rng.choice(np.array([4, 8, 16]), 8))])
def near(rng, b, n):
    i = (np.arange(16)[:, None] + rng.integers(0, 16, (N, 8, 1, n))) % 16
    v = np.take_along_axis(np.broadcast_to(b[None, :, :, None], (N, 8, 16, n)), i, 2)
    s = rng.integers(1, 25, (N, 8, 1, n))
    return np.clip(v + np.rint(s * (2 * rng.random((N, 8, 16, n)) - 1)).astype(np.int64), 0, 255)
def parts(rng):
    b = pattern(rng); x = near(rng, b, V); x = np.where(rng.random((N, 8, 1, V)) < 0.1, rng.integers(0, 256, x.shape), x); c = near(rng, b, CH)
    h = rng.integers(0, V, (N, 8, 16, HB)); h[rng.random(h.shape) < 0.15] = V
    l = rng.integers(0, V, (N, 8, 16, V)); l[rng.random(l.shape) < 0.25] = V
    return x, h, l, c, rng.integers(0, 256, (8, 16, 16)), rng.integers(80, 400, (N, 8, 16))
def pack(x, h, l, c, w, t):
    return {"xr": np.ascontiguousarray(x.reshape(N, 128, V)).astype(np.float32).astype(BF), "hd": np.ascontiguousarray(h.reshape(N, 128, HB)).astype(np.int32),
            "nx": np.ascontiguousarray(l.reshape(N, 128, V)).astype(np.int32), "c0": np.ascontiguousarray(c.reshape(N, 128, CH)).astype(np.float32).astype(BF),
            "wt": np.tile(w.reshape(1, 128, 16), (N, 1, 1)).astype(np.float32).astype(BF), "th": np.ascontiguousarray(t.reshape(N, 128, 1)).astype(np.int32)}
def setup_inputs(rng):
    return pack(*parts(rng))
def setup_inputs_crowd(rng):
    x, h, l, c, w, t = parts(rng)
    c[:, ::2] = np.take_along_axis(c, rng.integers(0, 5, (N, 8, 1, CH)), 3)[:, ::2]
    few = np.concatenate([np.array([0, V - 1]), 1 + rng.permutation(V - 2)[:30]])
    h[:, 1::2] = rng.choice(few, (N, 4, 16, HB))
    return pack(x, h, l, c, w, t)
def setup_inputs_ties(rng):
    x, h, l, c, w, t = parts(rng)
    t = rng.choice(np.array([0, 1, 15, 16, 17, 100, 250, 400]), (N, 8, 16)); x[:, ::2] = rng.integers(0, 256, (N, 4, 16, V))
    e = rng.integers(0, 2, (N, 2, 16, 1)) == 1; a = rng.integers(0, 16, (N, 2, 16, CH)); b = rng.integers(0, 16, (N, 2, 16, V))
    c[:, 2::4] = np.roll(np.where(e, 255 - a, a), 1, axis=2); x[:, 2::4] = np.where(e, b, 255 - b); t[:, 2::4] = rng.integers(1500, 3501, (N, 2, 16))
    dd = np.roll(c, -1, axis=2); k = places(w[None], dd); cc = np.arange(CH)
    for q in range(N):
        for g in range(8):
            o = rng.permutation(V)[:8 * CH].reshape(CH, 8); ds = np.argsort(rng.random((CH, 16)), axis=1)[:, :8]; hg, lg, xg, dg = h[q, g], l[q, g], x[q, g], dd[q, g]
            for j in range(8):
                d = ds[:, j]; rd = o[:, j]; at = k[q, g][d, cc]
                if j < 4: hg[d, at] = rd
                else:
                    e = hg[d, at]
                    if LV == 3 and j >= 6: e = np.where(e < V, lg[d, np.minimum(e, V - 1)], V)
                    m = e < V; lg[d[m], e[m]] = rd[m]
                far = np.maximum(t[q, g][d] + rng.integers(-1, 2, CH), 0)
                z = np.minimum(rng.integers(0, 9, (16, CH)), (far // 16)[None, :])
                step = (far // 16)[None, :] + (np.argsort(rng.random((16, CH)), axis=0) < (far % 16)[None, :]) + z - np.roll(z, 1, axis=0)
                xg[:, rd] = dg + np.where(dg < 128, 1, -1) * step
    return pack(x, h, l, c, w, t)
def setup_inputs_ends(rng):
    x, h, l, c, w, t = parts(rng); m = V // 2
    h[:, 0, :15] = V
    l[:, 1] = V
    x[:, 2:4, :, :m] = rng.integers(0, 256, (N, 2, 16, m)); h[:, 2:4] = rng.integers(0, m, (N, 2, 16, HB)); l[:, 2:4] = rng.integers(m, V, (N, 2, 16, V)); l[:, 3, :15] = V
    h[:, 4] = rng.choice(np.array([0, V - 1, V]), (N, 16, HB)); h[:, 4, 0] = 0; h[:, 4, 1] = V - 1; l[:, 4, :, 0] = V - 1; l[:, 4, :, V - 1] = 0
    x[:, 4, :, 0] = np.roll(c[:, 4, :, 0], -1, axis=1); x[:, 4, :, V - 1] = np.roll(c[:, 4, :, CH - 1], -1, axis=1)
    h[:, 5] = V
    l[:, 6] = np.arange(V)
    return pack(x, h, l, c, w, t)
def setup_inputs_eager(rng):
    x, h, l, c, w, t = parts(rng)
    x = rng.integers(0, 256, x.shape); c = rng.integers(0, 256, c.shape); t[:] = 4080
    x[:, 0] = 255 * rng.integers(0, 2, (N, 1, V)); c[:, 0] = 255 * rng.integers(0, 2, (N, 1, CH)); t[:, 0] = 4079 + rng.integers(0, 2, (N, 16))
    w[0] = 255; w[1] = 0; w[2] = rng.choice(np.array([0, 1, 255]), (16, 16)); t[:, 3] = 4079
    return pack(x, h, l, c, w, t)
def setup_inputs_spread(rng):
    x, h, l, c, w, t = parts(rng)
    x = np.minimum((np.exp2(8 * rng.random((N, 8, 1, V))) * rng.random((N, 8, 16, V))).astype(np.int64), 255)
    c = np.minimum((np.exp2(8 * rng.random((N, 8, 1, CH))) * rng.random((N, 8, 16, CH))).astype(np.int64), 255)
    w = np.minimum((np.exp2(8 * rng.random((8, 1, 16))) * (0.5 + 0.5 * rng.random((8, 16, 16)))).astype(np.int64), 255)
    t = np.minimum(np.exp2(12 * rng.random((N, 8, 16))).astype(np.int64), 4080)
    p = 1 + 2 * rng.random((N, 8, 16, 1))
    h = np.where(h == V, V, np.minimum((V * rng.random(h.shape) ** p).astype(np.int64), V - 1))
    l = np.where(l == V, V, np.minimum((V * rng.random(l.shape) ** p).astype(np.int64), V - 1))
    return pack(x, h, l, c, w, t)
def check_inputs(d):
    bad = []
    for k, lo, hi in (("xr", 0, 255), ("hd", 0, V), ("nx", 0, V), ("c0", 0, 255), ("wt", 0, 255), ("th", 0, 4080)):
        v = np.asarray(d[k]).astype(np.float64)
        if not bool(np.all((v >= lo) & (v <= hi))): bad.append("range of " + k)
        elif bool(np.any(v != np.floor(v))): bad.append("whole numbers in " + k)
    v = np.asarray(d["wt"]).astype(np.float64)
    if bool(np.any(v != v[:1])): bad.append("wt alike on all ranks")
    return bad
def reference(xr, hd, nx, c0, wt, th):
    x = np.concatenate([xr.astype(np.float32).astype(np.int64).reshape(N, 8, 16, V), np.full((N, 8, 16, 1), 512, np.int64)], axis=3)
    h = hd.astype(np.int64).reshape(N, 8, 16, HB); l = np.concatenate([nx.astype(np.int64).reshape(N, 8, 16, V), np.full((N, 8, 16, 1), V, np.int64)], axis=3)
    c = c0.astype(np.float32).astype(np.int64).reshape(N, 8, 16, CH); w = wt.astype(np.float32).astype(np.int64).reshape(N, 8, 16, 16)
    lim = np.tile(th.astype(np.int64).reshape(N, 8, 16), (1, 1, LV))[..., None]; low = np.tri(CH, k=-1, dtype=bool); took = np.zeros((N, 8, RO, CH), np.int64)
    for t in range(RO):
        dd = np.roll(c, -1, axis=2)
        cand = [np.take_along_axis(h, places(w, dd), 3)]
        for i in range(1, LV): cand.append(np.take_along_axis(l, cand[-1], 3))
        cd = np.concatenate(cand, axis=2)
        v = np.take_along_axis(x, cd.reshape(N, 8, 1, 16 * LV * CH), 3).reshape(N, 8, 16, 16 * LV, CH)
        good = np.add.reduce(np.abs(v - dd[:, :, :, None, :]), axis=2) <= lim
        first = np.argmax(good, axis=2)[:, :, None, :]
        rd = np.where(np.any(good, axis=2), np.take_along_axis(cd, first, 2)[:, :, 0], V)
        lost = np.any((rd[..., :, None] == rd[..., None, :]) & low, axis=-1)
        win = (rd < V) & ~lost; rd = np.where(win, rd, V); took[:, :, t] = rd
        c = np.where(win[:, :, None, :], (3 * dd + np.take_along_axis(x, rd[:, :, None, :], 3)) >> 2, dd)
        np.put_along_axis(x, rd[:, :, None, :], 512, 3)
        c = np.roll(c, 1 + t % (N - 1), axis=0)
    return {"yc": c.reshape(N, 128, CH).astype(np.float32), "yt": took.reshape(N, 8, RO * CH).astype(np.float32)}

@@ -1,0 +1,527 @@
+import math
+from concourse.mybir import AluOpType as ALU, ActivationFunctionType as AF
+
+V, HB, CH, RO = 1792, 1024, 96, 4
+XW = V + CH
+FAR = 1024.0
+BIG = 4096.0
+
+CFG = {
+    "H": [32, 32, 32], "L": [32, 64],
+    "xb": [[(32, "a"), (32, "v"), (16, "a"), (16, "v")], [(16, "a"), (16, "v"), (32, "v"), (16, "v"), (16, "v")]],
+    "sumb": 64, "byu": True, "cuts": 8, "tries": 5000, "seed": 1,
+    "bank": {"s": "b0", "u": "b1", "DT": "b5", "D": "b6", "ca": "b5", "cb": "b6", "da": "b0", "db1": "b1", "db2": "b0", "va": "b7",
+             "vb": "b7", "cnt": "b1", "M": "b2", "r": "b3", "S": "b4", "z": "b5", "Y": "b6", "M2": "b5", "kb": "b0"},
+    "cyc": 1.0, "gam": 1.5, "pe": 0.42, "wake": 60.0, "fix": 30.0, "rem": 2300.0, "rissue": 600.0, "bw": 200.0,
+    "vary": [{}, {"pe": 0.65}, {"gam": 1.15}, {"gam": 1.95}, {"wake": 150.0}],
+}
+MP = 0
+CHAINED = ("b2", "b3", "b4", "b7")
+
+
+def _sb(n, d):
+    return ("sbuf", [128, n], d)
+
+
+F32, BF, F16, I32, U16 = "float32", "bfloat16", "float16", "int32", "uint16"
+SCRATCH = {
+    "hds": _sb(HB, I32), "nxs": _sb(V + 8, I32), "xw": _sb(XW, BF), "c0s": _sb(CH, BF), "wts": _sb(16, BF), "ths": _sb(4, I32),
+    "hdf": _sb(HB, F32), "hu": _sb(4096, F32), "JU": _sb(256, F32), "usq": _sb(256, F32), "ui": _sb(256, I32), "uj": _sb(256, I32),
+    "offu": _sb(256, U16), "b16": _sb(4, F32),
+    "thf": _sb(4, F32), "pi": _sb(16, I32), "pa": _sb(16, I32), "pb": _sb(4, I32), "ab": _sb(16, BF), "cols": _sb(8, BF),
+    "J": _sb(144, BF), "Jg": _sb(128, BF), "J16": _sb(CH, BF), "JE": _sb(512, BF), "E": _sb(512, BF),
+    "PT": _sb(128, BF), "PR": _sb(128, BF), "I": _sb(128, BF), "B": _sb(128, BF), "NB": _sb(128, BF), "B16": _sb(128, F16),
+    "N4": _sb(128, F16), "IB": _sb(128, BF), "I32": _sb(128, F32), "Lm": _sb(128, BF), "Lt": _sb(128, BF),
+    "Lu": _sb(128, BF), "W": _sb(128, BF), "Z": _sb(144, BF), "dm": _sb(16, BF), "DG": _sb(2048, F16),
+    "OD": _sb(CH, BF), "OD2": _sb(CH, BF), "RSB": _sb(CH, F32), "DM0": _sb(CH, F32), "tmp": _sb(5 * CH, F32),
+    "thr": _sb(CH, F32), "wT": _sb(CH, F32), "far": _sb(CH, BF),
+    "kp": _sb(CH, F16), "ysq": _sb(CH, F32), "yi": _sb(CH, I32), "yj": _sb(CH, I32),
+    "offh": _sb(CH, U16), "offa": _sb(CH, U16), "offb": _sb(CH, U16), "offc": _sb(8, U16), "offt": _sb(8, U16),
+    "DT": _sb(384, BF), "GH": _sb(1536, F16), "GL": _sb(1536, F16), "Drep": _sb(1536, BF),
+    "xa": _sb(1536, BF), "xb": _sb(1536, BF), "aa": _sb(1536, BF), "bb": _sb(1536, BF),
+    "cand": _sb(2 * CH, F32), "near": _sb(2 * CH, BF), "sel": _sb(2 * CH, F16), "rT": _sb(CH, F32), "rT2": _sb(CH, F32),
+    "EQ": _sb(7 * CH, BF), "xc": _sb(CH, BF), "k1": _sb(CH, BF),
+    "Ds": _sb(RO * CH, BF), "ts": _sb(RO * CH, BF), "Dl": _sb(RO * CH, BF), "tl": _sb(RO * CH, BF), "nl": _sb(CH, BF),
+    "tk": _sb(RO * CH, F32), "yts": _sb(RO * CH, F32), "ycs": _sb(CH, F32),
+}
+for _k in range(8):
+    SCRATCH["b%d" % _k] = ("psum", [128, 512], F32)
+SEMAPHORES = (["cv", "ca", "cp", "cg", "sent", "l_c0", "l_wt", "l_th", "l_hd", "l_xr", "l_nx", "s_yt", "s_yc"]
+              + ["a%s%d" % (_x, _k) for _x in "DT" for _k in range(RO)])
+_ORDER = {}
+
+
+def depends(ops):
+    by, last, dma, deps = {}, {}, 0.0, []
+    for i, o in enumerate(ops):
+        dep = set(o["after"])
+        for (name, lo, hi, w) in o["acc"]:
+            dep.update(j for (j, l2, h2, w2) in by.get(name, []) if (w or w2) and l2 < hi and lo < h2)
+        for (name, lo, hi, w) in o["acc"]:
+            if w:
+                by[name] = [e for e in by.get(name, []) if not (lo <= e[1] and e[2] <= hi)]
+            by.setdefault(name, []).append((i, lo, hi, w))
+        for b in o["banks"]:
+            if o["q"] == "p" and b in CHAINED:
+                dep.update(last.get(b, ()))
+                last[b] = (i,)
+        dep.discard(i)
+        deps.append(sorted(dep))
+        if o["bytes"]:
+            dma = max(dma, 1700.0) + o["bytes"] / CFG["bw"]
+            o["lat"] = dma + 300.0
+    return [(o["q"], o["lat"], o["busy"], o["banks"], [(j, 0.0 if o["q"] == "p" == ops[j]["q"] else CFG["wake"]) for j in d])
+            for o, d in zip(ops, deps)], CFG["wake"]
+
+
+def place_calls(calls, wake, succ, prio):
+    n = len(calls)
+    left, start, done, eng, bank = [len(c[4]) for c in calls], [0.0] * n, [0.0] * n, {}, {}
+    ready = [i for i in range(n) if not left[i]]
+    while ready:
+        i = max(ready, key=lambda k: prio[k])
+        ready.remove(i)
+        q, lat, busy, banks, dep = calls[i]
+        t = 0.0
+        for j, w in dep:
+            if done[j] + w > t:
+                t = done[j] + w
+        if q != "x":
+            iv, moved = eng.setdefault(q, []), True
+            while moved:
+                moved = False
+                for (a, b) in iv:
+                    if t < b and a < t + busy:
+                        t, moved = b, True
+                for bk in banks:
+                    for (a, b, q2) in bank.get(bk, ()):
+                        if t < b + wake and q2 != q and a < t + lat + wake:
+                            t, moved = b + wake, True
+            iv.append((t, t + busy))
+            if len(iv) > 60:
+                iv.sort()
+                del iv[:20]
+                iv[0] = (0.0, iv[0][1])
+            for bk in banks:
+                bank.setdefault(bk, []).append((t, t + lat, q))
+        start[i], done[i] = t, t + lat
+        for j in succ[i]:
+            left[j] -= 1
+            if not left[j]:
+                ready.append(j)
+    return sorted(range(n), key=lambda k: (start[k], k))
+
+
+def span(calls, wake, order):
+    free, done, bank = {}, [0.0] * len(calls), {}
+    for i in order:
+        q, lat, busy, banks, dep = calls[i]
+        t = free.get(q, 0.0) if q != "x" else 0.0
+        for j, w in dep:
+            if done[j] + w > t:
+                t = done[j] + w
+        for b in banks:
+            for q2, t2 in bank.setdefault(b, {}).items():
+                if q2 != q and t2 + wake > t:
+                    t = t2 + wake
+        done[i], free[q] = t + lat, t + busy
+        for b in banks:
+            bank[b][q] = done[i]
+    return max(done)
+
+
+def schedule(make):
+    base, sets = dict(CFG), []
+    for m in base["vary"]:
+        CFG.update(m)
+        ops = make()
+        sets.append(depends(ops))
+        CFG.update(base)
+    calls, wake = sets[0]
+    n, succ, kinds, seen, r = len(calls), [[] for c in calls], {}, {}, [CFG["seed"]]
+    for i, c in enumerate(calls):
+        for j, w in c[4]:
+            succ[j].append(i)
+        seen[ops[i]["tag"]] = seen.get(ops[i]["tag"], 0) + 1
+        kinds.setdefault((ops[i]["tag"][1], seen[ops[i]["tag"]]), []).append(i)
+    keys = sorted(kinds, key=lambda k: kinds[k][0])
+
+    def rnd():
+        r[0] = (r[0] * 6364136223846793005 + 1442695040888963407) % 2 ** 64
+        return (r[0] >> 11) / 2.0 ** 53
+
+    def judge(p):
+        order = place_calls(calls, wake, succ, p)
+        return order, [span(c, w, order) for c, w in sets]
+
+    prio = [-100.0 * i for i in range(n)]
+    order, ref = judge(prio)
+    cur, best, spans = 1.0, 1.0, ref
+    for it in range(CFG["tries"]):
+        p, d, run = list(prio), (rnd() + rnd() - 1) * (500, 1500, 5000)[int(3 * rnd())], (1, 1, 3, 8, 20)[int(5 * rnd())]
+        if rnd() < 0.5:
+            x = int(n * rnd())
+            for i in range(max(x, 6), min(n, x + run)):
+                p[i] += d
+        else:
+            x = 6 + int((len(keys) - 6) * rnd())
+            for k in keys[x:x + run]:
+                for i in kinds[k]:
+                    p[i] += d
+        o2, v = judge(p)
+        s = sum(a / b for a, b in zip(v, ref)) / len(ref)
+        if s <= cur or rnd() < math.exp((cur - s) / (1e-6 + 0.001 * (1 - it / CFG["tries"]))):
+            cur, prio = s, p
+            if s < best:
+                best, order, spans = s, o2, v
+    return order, spans
+
+
+def build(g, core, T, topo, rank):
+    n_ranks = len(T.cores)
+    Q = {"a": g.scalar, "s": g.sync}
+    ops, tag = [], [(-1, "setup")]
+    cyc, fix = CFG["cyc"], CFG["fix"]
+
+    def S(name, lo=0, hi=None, step=1, p1=128):
+        t = T[name]
+        if hi is None:
+            hi = t.shape[1]
+        ap = t[0:p1, lo:hi] if step == 1 else t[0:p1, lo:hi:step]
+        return (ap, [(name, lo, hi)], (hi - lo + step - 1) // step, False)
+
+    def IND(win, off):
+        return (win[0].indirect(off[0]), win[1] + off[1], 16 * off[2], True)
+
+    def op(q, issue, reads, writes, lat, busy=None, sem=None, inc=1, after=(), nbytes=0, own=True):
+        acc = [r + (False,) for x in reads for r in x[1]] + [r + (True,) for x in writes for r in x[1]]
+        ops.append({"q": q, "issue": issue, "acc": acc, "lat": lat, "busy": lat if busy is None else busy, "sem": sem or "c" + q,
+                    "inc": inc, "after": after, "bytes": nbytes, "own": own, "tag": tag[0],
+                    "banks": sorted(set(a[0] for a in acc if SCRATCH[a[0]][0] == "psum"))})
+        return len(ops) - 1
+
+    def cost(out, ins, mul=1.0):
+        if ins[0][3]:
+            return 55 + out[2] * CFG["gam"] * cyc
+        if mul == 0.5 and any(SCRATCH[x[1][0][0]][2] in (F32, I32) for x in ins + [out]):
+            mul = 1.0
+        return fix + max(64, out[2] * mul) * cyc
+
+    def col(x):
+        return x[0] if isinstance(x, tuple) else x
+
+    def ts(out, in0, s1, op0, s2=None, op1=None):
+        ins = [x for x in (in0, s1, s2) if isinstance(x, tuple)]
+        if op1 is None:
+            op("v", lambda: g.vector.tensor_scalar(out[0], in0[0], col(s1), None, op0), ins, [out], cost(out, ins, 0.5))
+        else:
+            op("v", lambda: g.vector.tensor_scalar(out[0], in0[0], col(s1), col(s2), op0, op1), ins, [out], cost(out, ins, 0.5))
+
+    def tt(out, a, b, o):
+        both = SCRATCH[a[1][0][0]][0] == SCRATCH[b[1][0][0]][0]
+        op("v", lambda: g.vector.tensor_tensor(out[0], a[0], b[0], o), [a, b], [out], cost(out, [a, b], 2.0 if both else 1.0))
+
+    def cp(out, a):
+        op("v", lambda: g.vector.tensor_copy(out[0], a[0]), [a], [out], cost(out, [a], 0.5))
+
+    def scan(out, d0, d1, init, o0, o1):
+        op("v", lambda: g.vector.tensor_tensor_scan(out[0], d0[0], d1[0], init, o0, o1), [d0, d1], [out], cost(out, [d0]))
+
+    def fill(out, c):
+        op("v", lambda: g.vector.memset(out[0], c), [], [out], cost(out, [out], 0.5))
+
+    def act(out, a, f, bias=0.0, scale=1.0):
+        ins = [x for x in (a, bias) if isinstance(x, tuple)]
+        op("a", lambda: g.scalar.activation(out[0], a[0], f, bias=col(bias), scale=scale), ins, [out], cost(out, [a]))
+
+    def mm(out, pairs, start=True, stop=True):
+        def issue():
+            for k, (l, r) in enumerate(pairs):
+                ins = g.tensor.matmul(out[0], l[0], r[0], start and k == 0, stop and k == len(pairs) - 1)
+            return ins
+        c = sum(max(min(64, l[2]), r[2]) * (4 if SCRATCH[r[1][0][0]][2] == F32 else 1) for l, r in pairs) * CFG["pe"]
+        op("p", issue, [x for pr in pairs for x in pr], [out], c)
+
+    def iota(out, pattern, mult):
+        if SCRATCH[out[1][0][0]][2] == I32:
+            op("g", lambda: g.iota(out[0], pattern, 0, mult), [], [out], 130 + 2 * out[2] * cyc)
+        else:
+            op("g", lambda: g.iota(out[0], pattern, 0, mult, allow_small_or_imprecise_dtypes=True), [], [out], 130 + 2 * out[2] * cyc)
+
+    def load(q, sem, out, src, nbytes):
+        op(q, lambda: Q[q].dma_start(out[0], src), [], [out], 2000.0, 50.0, sem, 16, nbytes=nbytes)
+
+    def move(src, dst, sem, t):
+        to = T.cores[(rank + 1 + t % (n_ranks - 1)) % n_ranks]
+        frm = T.cores[(rank - 1 - t % (n_ranks - 1)) % n_ranks]
+        rid, pid = topo.addr(to, core)
+        i = op("g", lambda: g.remote_dma(dst[0], src[0], T.sem[sem], T.sem["sent"], pid, rid, topo.mask(core, to)), [src], [],
+               CFG["rissue"], None, "sent", len(topo.engines(core, to)), own=False)
+        op("x", None, [], [dst], CFG["rem"] - CFG["rissue"], 0.0, sem, len(topo.engines(frm, core)), after=(i,), own=False)
+
+    def places(out, sq, a, b):
+        ts(a, sq, 1.0 / 32, ALU.mult, -8.40625, ALU.add)
+        ts(b, a, HB - 1, ALU.bitwise_and)
+        cp(out, b)
+
+    load("s", "l_c0", S("c0s"), T.c0[:], 1)
+    load("a", "l_wt", S("wts"), T.wt[:], 1)
+    load("s", "l_hd", S("hds"), T.hd[:], 128 * HB * 4)
+    load("a", "l_th", S("ths", 0, 1), T.th[:], 1)
+    load("s", "l_xr", S("xw", 0, V), T.xr[:], 128 * V * 2)
+    load("s", "l_nx", S("nxs", 0, V), T.nx[:], 128 * V * 4)
+
+    iota(S("pi"), [[1, 16]], 1)
+    iota(S("J"), [[1, 144]], 0)
+    iota(S("Jg"), [[16, 8], [0, 16]], 0)
+    iota(S("JE"), [[1, 32], [0, 16]], 0)
+    iota(S("J16"), [[0, 6], [1, 16]], 0)
+    i16, nx16, pv16 = S("ab", 0, 1), S("ab", 1, 2), S("ab", 15, 16)
+    g16, pcol, J128 = S("cols", 0, 1), S("cols", 2, 3), S("J", 0, 128)
+    ts(S("pa"), S("pi"), 15, ALU.bitwise_and)
+    cp(S("ab"), S("pa"))
+    tt(g16, S("pi", 0, 1), S("pa", 0, 1), ALU.subtract)
+    ts(S("PT"), J128, g16, ALU.subtract, nx16, ALU.is_equal)
+    ts(S("B"), S("Jg"), g16, ALU.is_equal)
+    for k in range(8):
+        mm(S("b7", 16 * k, 16 * k + 16), [(S("PT"), S("wts"))])
+    tt(S("W"), S("b7", 0, 128), S("B"), ALU.mult)
+    cp(pcol, S("pi", 0, 1))
+    ts(S("N4"), J128, pcol, ALU.is_equal, -4096.0, ALU.mult)
+    ts(S("PR"), J128, g16, ALU.subtract, pv16, ALU.is_equal)
+    ts(S("I"), J128, pcol, ALU.is_equal)
+    ts(S("dm"), S("J", 0, 16), i16, ALU.is_equal, -1.0, ALU.mult)
+
+    def early():
+        for d in range(16):
+            ts(S("DG", 128 * d, 128 * d + 128), S("I"), S("dm", d, d + 1), ALU.mult)
+        ts(S("E"), S("JE"), pcol, ALU.is_equal)
+        fill(S("xw", V, XW), FAR)
+        fill(S("nxs", V, V + 8), V)
+        ts(S("Z"), S("J"), g16, ALU.subtract, 15.0, ALU.is_equal)
+
+    def by_u():
+        iota(S("JU"), [[16, 256]], 0)
+        ts(S("b16", 0, 1), i16, 16.0, ALU.add)
+        act(S("usq"), S("JU"), AF.Square, bias=S("b16", 0, 1))
+        places(S("offu"), S("usq"), S("ui"), S("uj"))
+        cp(S("hdf"), S("hds"))
+
+    def late():
+        act(S("NB"), S("B"), AF.Identity, scale=-1.0)
+        act(S("IB"), S("I"), AF.Identity, scale=BIG)
+        act(S("I32"), S("I"), AF.Identity)
+        cp(S("thf", 0, 1), S("ths", 0, 1))
+        ts(S("Lt"), J128, pcol, ALU.is_gt)
+        cp(S("B16"), S("B"))
+        tt(S("Lu"), S("Lt"), S("B"), ALU.mult)
+        tt(S("Lm"), S("I"), S("Lu"), ALU.subtract)
+        ts(S("OD"), S("J16"), i16, ALU.not_equal, -BIG, ALU.mult)
+        act(S("OD2"), S("OD"), AF.Identity, bias=-BIG)
+        ts(S("RSB"), S("J16"), 0.0, ALU.not_equal, 2 * BIG, ALU.mult)
+        ts(S("tmp", 0, CH), S("J", 0, CH), i16, ALU.add, -1.0, ALU.mult)
+        tt(S("DM0"), S("tmp", 0, CH), S("RSB"), ALU.add)
+        fill(S("tmp", CH, 2 * CH), 0.5)
+        fill(S("tmp", 2 * CH, 3 * CH), 0.0)
+        scan(S("thr"), S("tmp", CH, 2 * CH), S("tmp", 2 * CH, 3 * CH), 2.0, ALU.mult, ALU.add)
+        ts(S("tmp", 3 * CH, 4 * CH), S("J16"), i16, ALU.is_equal, 0.5, ALU.mult)
+        tt(S("tmp", 4 * CH, 5 * CH), S("tmp", 3 * CH, 4 * CH), S("thr"), ALU.mult)
+        scan(S("wT"), S("RSB"), S("tmp", 4 * CH, 5 * CH), 0.0, ALU.min, ALU.max)
+        fill(S("EQ"), 0.0)
+        fill(S("far"), FAR)
+
+    xwin = S("xw")
+    place, used = {}, {}
+    for name in sorted(CFG["bank"]):
+        b = CFG["bank"][name]
+        place[name] = used.get(b, 0)
+        used[b] = place[name] + (128 if name == "DT" else CH)
+
+    def P(name, c0=0, c1=CH, p1=128):
+        return S(CFG["bank"][name], place[name] + c0, place[name] + c1, p1=p1)
+
+    def big(name, c0, c1):
+        return S(name, 16 * c0, 16 * c1)
+
+    def rep(c0, c1, stop):
+        j = c0 // 32
+        lo, hi = 16 * (c0 - 32 * j), 16 * (c1 - 32 * j)
+        R = S("b%d" % (2 + j), lo, hi)
+        rows = slice(32 * j, 32 * j + 32)
+        mm(R, [((T.DT[rows, 0:128], [("DT", 0, 128)], 128, False), (T.E32[rows, lo:hi], [("E32", lo, hi)], hi - lo, False))], stop=stop)
+        return R
+
+    def column_gather(c0, c1, q, off, xn, an):
+        if q == "a":
+            act(big(xn, c0, c1), IND(xwin, S(off, c0, c1)), AF.Identity, scale=-1.0)
+            R = rep(c0, c1, False)
+            mm(R, [(S("I"), big(xn, c0, c1))], start=False)
+            act(big(an, c0, c1), R, AF.Abs)
+        else:
+            tt(big(xn, c0, c1), IND(xwin, S(off, c0, c1)), big("Drep", c0, c1), ALU.subtract)
+            act(big(an, c0, c1), big(xn, c0, c1), AF.Abs)
+
+    def rowsum(out, an, c0, c1):
+        mm(out, [(S("Z", 15 - d, 143 - d), S(an, 16 * c0 + d, 16 * c1, 16)) for d in range(16)])
+
+    def pieces(ws):
+        return [(sum(ws[:k]), sum(ws[:k + 1])) for k in range(len(ws))]
+
+    for t in range(RO):
+        o, by = t * CH, t > 0 and CFG["byu"]
+        tag[0] = (t, "round")
+        C = [S("c0s")] if t == 0 else [S("Dl", o - CH, o), S("tl", o - CH, o)]
+        Ds, xb = S("Ds", o, o + CH), CFG["xb"][min(t, 1)]
+        xb = [p + (q,) for p, (w, q) in zip(pieces([w for w, q in xb]), xb)]
+        mm(P("s"), [(S("W"), c) for c in C])
+        ts(S("kp"), P("s"), 2.0 ** -12, ALU.mult, 1535.5 + 2.0 ** -13, ALU.add)
+        mm(P("u"), [(S("W"), c) for c in C] + [(S("N4"), S("kp"))])
+        if by:
+            ts(S("offh"), P("u"), 1536.0 * 4096, ALU.add)
+        else:
+            act(S("ysq"), P("u"), AF.Square, bias=1536.0 * 4096 + 16)
+            places(S("offh"), S("ysq"), S("yi"), S("yj"))
+        if t == 0:
+            early()
+            ts(S("pb", 0, 1), S("pi", 0, 1), 31, ALU.bitwise_and)
+            cp(S("cols", 4, 5), S("pb", 0, 1))
+            ts(S("E32"), S("JE"), S("cols", 4, 5), ALU.is_equal)
+        mm(P("DT", 0, 128, p1=CH), [(c, S("PR")) for c in C])
+        act(S("DT", 0, 128, p1=CH), P("DT", 0, 128, p1=CH), AF.Identity)
+        mm(P("D"), [(S("PR"), c) for c in C])
+        H, L = pieces(CFG["H"]), pieces(CFG["L"])
+        steps = ([(p, "GH", S("hu") if by else S("hds"), "offh", "ca", "offa") for p in H]
+                 + [(p, "GL", S("nxs"), "offa", "cb", "offb") for p in L])
+        for k, (p, G, win, offi, reg, offo) in enumerate(steps):
+            cp(big(G, *p), IND(win, S(offi, *p)))
+            if k > 0:
+                ts(S(steps[k - 1][5], *steps[k - 1][0]), P(steps[k - 1][4], *steps[k - 1][0]), -1.0, ALU.mult)
+            mm(P(reg, *p), [(S("DG", 128 * d, 128 * d + 128), S(G, 16 * p[0] + d, 16 * p[1], 16)) for d in range(16)])
+            if t == 0 and k == len(H) and CFG["byu"]:
+                by_u()
+        for j in range(3):
+            ws = [p for p in xb if p[2] == "v" and p[0] // 32 == j]
+            if ws:
+                act(big("Drep", ws[0][0], ws[-1][1]), rep(ws[0][0], ws[-1][1], True), AF.Identity)
+        act(Ds, P("D"), AF.Identity)
+        move(Ds, S("Dl", o, o + CH), "aD%d" % t, t)
+        for j in range(3):
+            column_gather(32 * j, 32 * j + 32, "a", "offa", "xa", "aa")
+        act(S("cand", 0, CH), P("ca"), AF.Identity)
+        rowsum(P("da"), "aa", 0, CH)
+        vs = [p for p in xb if p[2] == "v" and p[1] <= L[-1][0]][:1]
+        for p in vs:
+            column_gather(p[0], p[1], p[2], "offb", "xb", "bb")
+        ts(S("offb", *L[-1]), P("cb", *L[-1]), -1.0, ALU.mult)
+        for p in xb:
+            if p not in vs:
+                column_gather(p[0], p[1], p[2], "offb", "xb", "bb")
+        act(S("cand", CH, 2 * CH), P("cb"), AF.Identity)
+        if t == 0:
+            late()
+        m = CFG["sumb"]
+        rowsum(P("db2", m, CH), "bb", m, CH)
+        rowsum(P("db1", 0, m), "bb", 0, m)
+        na, nb, sa, sb, th = S("near", 0, CH), S("near", CH, 2 * CH), S("sel", 0, CH), S("sel", CH, 2 * CH), S("thf", 0, 1)
+        ts(na, P("da"), th, ALU.is_le, BIG, ALU.mult)
+        mm(P("va"), [(S("I32"), S("cand", 0, CH)), (S("Lm"), na)])
+        ts(sa, P("va"), V - BIG, ALU.add, 0.0, ALU.max)
+        mm(P("vb"), [(S("I32"), S("cand", CH, 2 * CH)), (S("NB"), na)], stop=False)
+        mm(P("M"), [(S("I"), S("OD")), (S("B16"), sa)], stop=False)
+        mm(P("r"), [(S("B16"), sa)], stop=False)
+        ts(S("near", CH + m, 2 * CH), P("db2", m, CH), th, ALU.is_le, BIG, ALU.mult)
+        ts(S("near", CH, CH + m), P("db1", 0, m), th, ALU.is_le, BIG, ALU.mult)
+        mm(P("vb"), [(S("Lm"), nb)], start=False)
+        ts(sb, P("vb"), V - BIG, ALU.add, 0.0, ALU.max)
+        mm(P("M"), [(S("B16"), sb)], start=False)
+        mm(P("r"), [(S("B16"), sb)], start=False)
+        scan(S("rT"), S("RSB"), P("M"), 0.0, ALU.min, ALU.max)
+        offc = S("offc", 0, 6)
+        ts(offc, S("rT", 15, CH, 16), -1.0, ALU.mult, float(V), ALU.add)
+        act(S("xc"), IND(xwin, offc), AF.Identity, scale=-1.0)
+        mm(P("z"), [(S("I"), Ds), (S("I"), S("xc"))])
+        act(S("k1"), P("z"), AF.Identity, bias=191.625, scale=-0.25)
+        act(P("kb"), S("k1"), AF.Identity, bias=-192.0)
+        mm(P("cnt"), [(S("B"), na), (S("B"), nb)])
+        act(S("EQ", 6 * CH, 7 * CH), P("cnt"), AF.Relu, bias=1.0, scale=-1.0)
+        mm(P("S"), [(S("B"), S("EQ", 6 * CH, 7 * CH))], stop=False)
+        for k in range(6):
+            ts(S("EQ", k * CH + 16 * k, (k + 1) * CH), P("r", 16 * k, CH), S("rT", 16 * k + 15, 16 * k + 16), ALU.is_equal,
+               S("wT", 16 * k + 15, 16 * k + 16), ALU.mult)
+            mm(P("S"), [(S("B"), S("EQ", k * CH, (k + 1) * CH))], start=False, stop=k == 5)
+        nl = S("nl")
+        tt(nl, P("S"), S("thr"), ALU.is_lt)
+        tt(S("ts", o, o + CH), nl, P("kb"), ALU.mult)
+        move(S("ts", o, o + CH), S("tl", o, o + CH), "aT%d" % t, t)
+        tag[0] = (t, "after")
+        both = [(S("B16"), sa), (S("B16"), sb), (S("IB"), nl)]
+        mm(P("Y"), both)
+        act(S("tk", o, o + CH), P("Y"), AF.Relu, bias=-BIG)
+        if t < RO - 1:
+            mm(P("M2"), [(S("I"), S("OD2"))] + both)
+            scan(S("rT2"), S("DM0"), P("M2"), 0.0, ALU.min, ALU.max)
+            ts(S("offt", 0, 6), S("rT2", 15, CH, 16), -1.0, ALU.mult, float(V), ALU.add)
+            ind = IND(xwin, S("offt", 0, 6))
+            op("v", lambda ind=ind: g.vector.tensor_copy(ind[0], T.far[:]), [S("far"), S("offt", 0, 6)], [xwin], 50 + 3 * CH * cyc)
+        if t == 0 and CFG["byu"]:
+            w = 256 // CFG["cuts"]
+            for k in range(CFG["cuts"]):
+                act(S("hu", 16 * w * k, 16 * w * (k + 1)), IND(S("hdf"), S("offu", w * k, w * (k + 1))), AF.Identity)
+
+    tag[0] = (RO, "out")
+    o = (RO - 1) * CH
+    tt(S("ycs"), S("Dl", o, o + CH), S("tl", o, o + CH), ALU.add)
+    op("s", lambda: g.sync.dma_start(T.yc[:], T.ycs[:]), [S("ycs")], [], 2000.0, 50.0, "s_yc", 16)
+    act(S("yts"), S("tk"), AF.Identity, bias=float(V), scale=-1.0)
+    op("a", lambda: g.scalar.dma_start(T.yt[:], T.yts[0:128:16, :]), [S("yts")], [], 2000.0, 50.0, "s_yt", 16)
+    return [x for x in ops]
+
+
+SCRATCH["E32"] = SCRATCH.pop("E")
+SCRATCH["E"] = _sb(512, BF)
+
+
+def rank_program(g, core, T, topo):
+    rank = T.rank_of(core)
+    if rank is None:
+        return
+    if "order" not in _ORDER:
+        _ORDER["order"], _ORDER["span"] = schedule(lambda: build(g, core, T, topo, rank))
+    ops = build(g, core, T, topo, rank)
+    Q = {"v": g.vector, "a": g.scalar, "p": g.tensor, "g": g, "s": g.sync}
+    count, waited, hist = {}, {}, {}
+    known = {q: {} for q in Q}
+
+    def wait(q, sem, n):
+        Q[q].wait_ge(T.sem[sem], n)
+        known[q][sem] = n
+        waited[sem] = max(waited.get(sem, 0), n)
+
+    for i in _ORDER["order"]:
+        o = ops[i]
+        q, sem, need = o["q"], o["sem"], {}
+        if q != "x":
+            for (name, lo, hi, wr) in o["acc"]:
+                bank = SCRATCH[name][0] == "psum"
+                for (l2, h2, w2, q2, tok, clock) in hist.get(name, []):
+                    if q2 == q == "p":
+                        continue
+                    if (((wr or w2) and l2 < hi and lo < h2) or (bank and q2 != q)) and need.get(tok[0], (0, None))[0] < tok[1]:
+                        need[tok[0]] = (tok[1], clock)
+            todo = [(s, n, c) for s, (n, c) in need.items() if known[q].get(s, 0) < n]
+            for s, n, c in [(s, n, c) for (s, n, c) in todo if not any(s2 != s and c2.get(s, 0) >= n for (s2, n2, c2) in todo)]:
+                wait(q, s, n)
+                for s2, n2 in c.items():
+                    known[q][s2] = max(known[q].get(s2, 0), n2)
+        count[sem] = count.get(sem, 0) + o["inc"]
+        if o["issue"] is not None:
+            ins = o["issue"]()
+            if o["own"]:
+                ins.then_inc(T.sem[sem], o["inc"])
+        tok, clock = (sem, count[sem]), dict(known.get(q, {}))
+        for (name, lo, hi, wr) in o["acc"]:
+            old = [e for e in hist.get(name, []) if not (e[3] == q and e[4][0] == sem and e[0] == lo and e[1] == hi and e[2] == wr)]
+            hist[name] = old + [(lo, hi, wr, q, tok, clock)]
+    for sem in SEMAPHORES:
+        if waited.get(sem, 0) < count.get(sem, 0):
+            wait("g", sem, count[sem])

@@ -8,14 +8,14 @@ BIG = 4096.0
 
 CFG = {
     "H": [32, 32, 32], "L": [32, 64],
-    "xb": [[(32, "a"), (32, "v"), (16, "a"), (16, "v")], [(16, "a"), (16, "v"), (32, "v"), (16, "v"), (16, "v")]],
-    "sumb": 64, "byu": True, "cuts": 8, "tries": 5000, "seed": 1,
+    "xa": [[(32, "a"), (32, "a"), (32, "v")], [(32, "a"), (32, "a"), (32, "a")]],
+    "xb": [[(32, "v"), (32, "v"), (16, "v"), (16, "v")], [(16, "a"), (16, "v"), (32, "v"), (24, "v"), (8, "v")]],
+    "sumb": 64, "byu": True, "cuts": 8, "tries": 8500, "seed": 3,
     "bank": {"s": "b0", "u": "b1", "DT": "b5", "D": "b6", "ca": "b5", "cb": "b6", "da": "b0", "db1": "b1", "db2": "b0", "va": "b7",
              "vb": "b7", "cnt": "b1", "M": "b2", "r": "b3", "S": "b4", "z": "b5", "Y": "b6", "M2": "b5", "kb": "b0"},
-    "cyc": 1.0, "gam": 1.5, "pe": 0.42, "wake": 60.0, "fix": 30.0, "rem": 2300.0, "rissue": 600.0, "bw": 200.0,
-    "vary": [{}, {"pe": 0.65}, {"gam": 1.15}, {"gam": 1.95}, {"wake": 150.0}],
+    "cyc": 0.83, "gam": 1.5, "pe": 0.42, "wake": 120.0, "fix": 30.0, "rem": 3200.0, "rissue": 700.0, "bw": 200.0,
+    "vary": [{}, {"pe": 0.6}, {"cyc": 1.15}],
 }
-MP = 0
 CHAINED = ("b2", "b3", "b4", "b7")
 
 
@@ -29,7 +29,7 @@ SCRATCH = {
     "hdf": _sb(HB, F32), "hu": _sb(4096, F32), "JU": _sb(256, F32), "usq": _sb(256, F32), "ui": _sb(256, I32), "uj": _sb(256, I32),
     "offu": _sb(256, U16), "b16": _sb(4, F32),
     "thf": _sb(4, F32), "pi": _sb(16, I32), "pa": _sb(16, I32), "pb": _sb(4, I32), "ab": _sb(16, BF), "cols": _sb(8, BF),
-    "J": _sb(144, BF), "Jg": _sb(128, BF), "J16": _sb(CH, BF), "JE": _sb(512, BF), "E": _sb(512, BF),
+    "J": _sb(144, BF), "Jg": _sb(128, BF), "J16": _sb(CH, BF), "JE": _sb(512, BF), "E32": _sb(512, BF),
     "PT": _sb(128, BF), "PR": _sb(128, BF), "I": _sb(128, BF), "B": _sb(128, BF), "NB": _sb(128, BF), "B16": _sb(128, F16),
     "N4": _sb(128, F16), "IB": _sb(128, BF), "I32": _sb(128, F32), "Lm": _sb(128, BF), "Lt": _sb(128, BF),
     "Lu": _sb(128, BF), "W": _sb(128, BF), "Z": _sb(144, BF), "dm": _sb(16, BF), "DG": _sb(2048, F16),
@@ -37,10 +37,10 @@ SCRATCH = {
     "thr": _sb(CH, F32), "wT": _sb(CH, F32), "far": _sb(CH, BF),
     "kp": _sb(CH, F16), "ysq": _sb(CH, F32), "yi": _sb(CH, I32), "yj": _sb(CH, I32),
     "offh": _sb(CH, U16), "offa": _sb(CH, U16), "offb": _sb(CH, U16), "offc": _sb(8, U16), "offt": _sb(8, U16),
-    "DT": _sb(384, BF), "GH": _sb(1536, F16), "GL": _sb(1536, F16), "Drep": _sb(1536, BF),
+    "DT": _sb(128, BF), "GH": _sb(1536, F16), "GL": _sb(1536, F16), "Drep": _sb(1536, BF),
     "xa": _sb(1536, BF), "xb": _sb(1536, BF), "aa": _sb(1536, BF), "bb": _sb(1536, BF),
     "cand": _sb(2 * CH, F32), "near": _sb(2 * CH, BF), "sel": _sb(2 * CH, F16), "rT": _sb(CH, F32), "rT2": _sb(CH, F32),
-    "EQ": _sb(7 * CH, BF), "xc": _sb(CH, BF), "k1": _sb(CH, BF),
+    "EQ": _sb(7 * CH, BF), "xq": _sb(CH, F32), "kk": _sb(CH, I32), "I4": _sb(128, BF),
     "Ds": _sb(RO * CH, BF), "ts": _sb(RO * CH, BF), "Dl": _sb(RO * CH, BF), "tl": _sb(RO * CH, BF), "nl": _sb(CH, BF),
     "tk": _sb(RO * CH, F32), "yts": _sb(RO * CH, F32), "ycs": _sb(CH, F32),
 }
@@ -70,8 +70,8 @@ def depends(ops):
         if o["bytes"]:
             dma = max(dma, 1700.0) + o["bytes"] / CFG["bw"]
             o["lat"] = dma + 300.0
-    return [(o["q"], o["lat"], o["busy"], o["banks"], [(j, 0.0 if o["q"] == "p" == ops[j]["q"] else CFG["wake"]) for j in d])
-            for o, d in zip(ops, deps)], CFG["wake"]
+    return [(o["q"], o["lat"], o["busy"], o["banks"], [(j, 0.0 if o["q"] == "p" == ops[j]["q"] else CFG["wake"]) for j in d]
+             + [(j, -ops[j]["lat"]) for j in ([o["order"]] if "order" in o else [])]) for o, d in zip(ops, deps)], CFG["wake"]
 
 
 def place_calls(calls, wake, succ, prio):
@@ -158,8 +158,8 @@ def schedule(make):
     order, ref = judge(prio)
     cur, best, spans = 1.0, 1.0, ref
     for it in range(CFG["tries"]):
-        p, d, run = list(prio), (rnd() + rnd() - 1) * (500, 1500, 5000)[int(3 * rnd())], (1, 1, 3, 8, 20)[int(5 * rnd())]
-        if rnd() < 0.5:
+        p, d, run = list(prio), (rnd() + rnd() - 1) * (300, 800, 2500)[int(3 * rnd())], (1, 1, 1, 2, 4)[int(5 * rnd())]
+        if rnd() < 0.3:
             x = int(n * rnd())
             for i in range(max(x, 6), min(n, x + run)):
                 p[i] += d
@@ -170,7 +170,7 @@ def schedule(make):
                     p[i] += d
         o2, v = judge(p)
         s = sum(a / b for a, b in zip(v, ref)) / len(ref)
-        if s <= cur or rnd() < math.exp((cur - s) / (1e-6 + 0.001 * (1 - it / CFG["tries"]))):
+        if s <= cur or rnd() < math.exp((cur - s) / (1e-6 + 0.0003 * (1 - it / CFG["tries"]))):
             cur, prio = s, p
             if s < best:
                 best, order, spans = s, o2, v
@@ -268,8 +268,8 @@ def build(g, core, T, topo, rank):
     load("a", "l_wt", S("wts"), T.wt[:], 1)
     load("s", "l_hd", S("hds"), T.hd[:], 128 * HB * 4)
     load("a", "l_th", S("ths", 0, 1), T.th[:], 1)
-    load("s", "l_xr", S("xw", 0, V), T.xr[:], 128 * V * 2)
     load("s", "l_nx", S("nxs", 0, V), T.nx[:], 128 * V * 4)
+    load("s", "l_xr", S("xw", 0, V), T.xr[:], 128 * V * 2)
 
     iota(S("pi"), [[1, 16]], 1)
     iota(S("J"), [[1, 144]], 0)
@@ -295,7 +295,6 @@ def build(g, core, T, topo, rank):
     def early():
         for d in range(16):
             ts(S("DG", 128 * d, 128 * d + 128), S("I"), S("dm", d, d + 1), ALU.mult)
-        ts(S("E"), S("JE"), pcol, ALU.is_equal)
         fill(S("xw", V, XW), FAR)
         fill(S("nxs", V, V + 8), V)
         ts(S("Z"), S("J"), g16, ALU.subtract, 15.0, ALU.is_equal)
@@ -306,11 +305,15 @@ def build(g, core, T, topo, rank):
         act(S("usq"), S("JU"), AF.Square, bias=S("b16", 0, 1))
         places(S("offu"), S("usq"), S("ui"), S("uj"))
         cp(S("hdf"), S("hds"))
+        w = 256 // CFG["cuts"]
+        for k in range(CFG["cuts"]):
+            act(S("hu", 16 * w * k, 16 * w * (k + 1)), IND(S("hdf"), S("offu", w * k, w * (k + 1))), AF.Identity)
 
     def late():
         act(S("NB"), S("B"), AF.Identity, scale=-1.0)
         act(S("IB"), S("I"), AF.Identity, scale=BIG)
         act(S("I32"), S("I"), AF.Identity)
+        act(S("I4"), S("I"), AF.Identity, scale=0.25)
         cp(S("thf", 0, 1), S("ths", 0, 1))
         ts(S("Lt"), J128, pcol, ALU.is_gt)
         cp(S("B16"), S("B"))
@@ -373,6 +376,8 @@ def build(g, core, T, topo, rank):
         C = [S("c0s")] if t == 0 else [S("Dl", o - CH, o), S("tl", o - CH, o)]
         Ds, xb = S("Ds", o, o + CH), CFG["xb"][min(t, 1)]
         xb = [p + (q,) for p, (w, q) in zip(pieces([w for w, q in xb]), xb)]
+        xa = CFG["xa"][min(t, 1)]
+        xa = [p + (q,) for p, (w, q) in zip(pieces([w for w, q in xa]), xa)]
         mm(P("s"), [(S("W"), c) for c in C])
         ts(S("kp"), P("s"), 2.0 ** -12, ALU.mult, 1535.5 + 2.0 ** -13, ALU.add)
         mm(P("u"), [(S("W"), c) for c in C] + [(S("N4"), S("kp"))])
@@ -397,16 +402,16 @@ def build(g, core, T, topo, rank):
             if k > 0:
                 ts(S(steps[k - 1][5], *steps[k - 1][0]), P(steps[k - 1][4], *steps[k - 1][0]), -1.0, ALU.mult)
             mm(P(reg, *p), [(S("DG", 128 * d, 128 * d + 128), S(G, 16 * p[0] + d, 16 * p[1], 16)) for d in range(16)])
-            if t == 0 and k == len(H) and CFG["byu"]:
+            if t == 0 and k == len(H) - 1 and CFG["byu"]:
                 by_u()
         for j in range(3):
-            ws = [p for p in xb if p[2] == "v" and p[0] // 32 == j]
+            ws = sorted(p for p in xa + xb if p[2] == "v" and p[0] // 32 == j)
             if ws:
-                act(big("Drep", ws[0][0], ws[-1][1]), rep(ws[0][0], ws[-1][1], True), AF.Identity)
+                act(big("Drep", ws[0][0], max(p[1] for p in ws)), rep(ws[0][0], max(p[1] for p in ws), True), AF.Identity)
         act(Ds, P("D"), AF.Identity)
         move(Ds, S("Dl", o, o + CH), "aD%d" % t, t)
-        for j in range(3):
-            column_gather(32 * j, 32 * j + 32, "a", "offa", "xa", "aa")
+        for p in xa:
+            column_gather(p[0], p[1], p[2], "offa", "xa", "aa")
         act(S("cand", 0, CH), P("ca"), AF.Identity)
         rowsum(P("da"), "aa", 0, CH)
         vs = [p for p in xb if p[2] == "v" and p[1] <= L[-1][0]][:1]
@@ -438,22 +443,24 @@ def build(g, core, T, topo, rank):
         scan(S("rT"), S("RSB"), P("M"), 0.0, ALU.min, ALU.max)
         offc = S("offc", 0, 6)
         ts(offc, S("rT", 15, CH, 16), -1.0, ALU.mult, float(V), ALU.add)
-        act(S("xc"), IND(xwin, offc), AF.Identity, scale=-1.0)
-        mm(P("z"), [(S("I"), Ds), (S("I"), S("xc"))])
-        act(S("k1"), P("z"), AF.Identity, bias=191.625, scale=-0.25)
-        act(P("kb"), S("k1"), AF.Identity, bias=-192.0)
+        act(S("xq"), IND(xwin, offc), AF.Identity, bias=-0.375, scale=0.25)
+        mm(P("z"), [(S("I4"), Ds)])
         mm(P("cnt"), [(S("B"), na), (S("B"), nb)])
         act(S("EQ", 6 * CH, 7 * CH), P("cnt"), AF.Relu, bias=1.0, scale=-1.0)
         mm(P("S"), [(S("B"), S("EQ", 6 * CH, 7 * CH))], stop=False)
         for k in range(6):
             ts(S("EQ", k * CH + 16 * k, (k + 1) * CH), P("r", 16 * k, CH), S("rT", 16 * k + 15, 16 * k + 16), ALU.is_equal,
                S("wT", 16 * k + 15, 16 * k + 16), ALU.mult)
+            if k:
+                ops[-1]["order"] = len(ops) - 3
             mm(P("S"), [(S("B"), S("EQ", k * CH, (k + 1) * CH))], start=False, stop=k == 5)
         nl = S("nl")
-        tt(nl, P("S"), S("thr"), ALU.is_lt)
-        tt(S("ts", o, o + CH), nl, P("kb"), ALU.mult)
+        tt(S("kk"), S("xq"), P("z"), ALU.subtract)
+        tt(P("kb"), P("S"), S("thr"), ALU.is_lt)
+        tt(S("ts", o, o + CH), S("kk"), P("kb"), ALU.mult)
         move(S("ts", o, o + CH), S("tl", o, o + CH), "aT%d" % t, t)
         tag[0] = (t, "after")
+        tt(nl, P("S"), S("thr"), ALU.is_lt)
         both = [(S("B16"), sa), (S("B16"), sb), (S("IB"), nl)]
         mm(P("Y"), both)
         act(S("tk", o, o + CH), P("Y"), AF.Relu, bias=-BIG)
@@ -463,10 +470,6 @@ def build(g, core, T, topo, rank):
             ts(S("offt", 0, 6), S("rT2", 15, CH, 16), -1.0, ALU.mult, float(V), ALU.add)
             ind = IND(xwin, S("offt", 0, 6))
             op("v", lambda ind=ind: g.vector.tensor_copy(ind[0], T.far[:]), [S("far"), S("offt", 0, 6)], [xwin], 50 + 3 * CH * cyc)
-        if t == 0 and CFG["byu"]:
-            w = 256 // CFG["cuts"]
-            for k in range(CFG["cuts"]):
-                act(S("hu", 16 * w * k, 16 * w * (k + 1)), IND(S("hdf"), S("offu", w * k, w * (k + 1))), AF.Identity)
 
     tag[0] = (RO, "out")
     o = (RO - 1) * CH
@@ -474,11 +477,7 @@ def build(g, core, T, topo, rank):
     op("s", lambda: g.sync.dma_start(T.yc[:], T.ycs[:]), [S("ycs")], [], 2000.0, 50.0, "s_yc", 16)
     act(S("yts"), S("tk"), AF.Identity, bias=float(V), scale=-1.0)
     op("a", lambda: g.scalar.dma_start(T.yt[:], T.yts[0:128:16, :]), [S("yts")], [], 2000.0, 50.0, "s_yt", 16)
-    return [x for x in ops]
-
-
-SCRATCH["E32"] = SCRATCH.pop("E")
-SCRATCH["E"] = _sb(512, BF)
+    return ops
 
 
 def rank_program(g, core, T, topo):

import math
from concourse.mybir import AluOpType as ALU, ActivationFunctionType as AF

V, HB, CH, RO = 1792, 1024, 96, 4
XW = V + CH
FAR = 1024.0
BIG = 4096.0

CFG = {
    "H": [32, 32, 32], "L": [32, 64],
    "xa": [[(32, "a"), (32, "a"), (32, "v")], [(32, "a"), (32, "a"), (32, "a")]],
    "xb": [[(32, "v"), (32, "v"), (16, "v"), (16, "v")], [(16, "a"), (16, "v"), (32, "v"), (24, "v"), (8, "v")]],
    "sumb": 64, "byu": True, "cuts": 8, "tries": 8500, "seed": 3,
    "bank": {"s": "b0", "u": "b1", "DT": "b5", "D": "b6", "ca": "b5", "cb": "b6", "da": "b0", "db1": "b1", "db2": "b0", "va": "b7",
             "vb": "b7", "cnt": "b1", "M": "b2", "r": "b3", "S": "b4", "z": "b5", "Y": "b6", "M2": "b5", "kb": "b0"},
    "cyc": 0.83, "gam": 1.5, "pe": 0.42, "wake": 120.0, "fix": 30.0, "rem": 3200.0, "rissue": 700.0, "bw": 200.0,
    "vary": [{}, {"pe": 0.6}, {"cyc": 1.15}],
}
CHAINED = ("b2", "b3", "b4", "b7")


def _sb(n, d):
    return ("sbuf", [128, n], d)


F32, BF, F16, I32, U16 = "float32", "bfloat16", "float16", "int32", "uint16"
SCRATCH = {
    "hds": _sb(HB, I32), "nxs": _sb(V + 8, I32), "xw": _sb(XW, BF), "c0s": _sb(CH, BF), "wts": _sb(16, BF), "ths": _sb(4, I32),
    "hdf": _sb(HB, F32), "hu": _sb(4096, F32), "JU": _sb(256, F32), "usq": _sb(256, F32), "ui": _sb(256, I32), "uj": _sb(256, I32),
    "offu": _sb(256, U16), "b16": _sb(4, F32),
    "thf": _sb(4, F32), "pi": _sb(16, I32), "pa": _sb(16, I32), "pb": _sb(4, I32), "ab": _sb(16, BF), "cols": _sb(8, BF),
    "J": _sb(144, BF), "Jg": _sb(128, BF), "J16": _sb(CH, BF), "JE": _sb(512, BF), "E32": _sb(512, BF),
    "PT": _sb(128, BF), "PR": _sb(128, BF), "I": _sb(128, BF), "B": _sb(128, BF), "NB": _sb(128, BF), "B16": _sb(128, F16),
    "N4": _sb(128, F16), "IB": _sb(128, BF), "I32": _sb(128, F32), "Lm": _sb(128, BF), "Lt": _sb(128, BF),
    "Lu": _sb(128, BF), "W": _sb(128, BF), "Z": _sb(144, BF), "dm": _sb(16, BF), "DG": _sb(2048, F16),
    "OD": _sb(CH, BF), "OD2": _sb(CH, BF), "RSB": _sb(CH, F32), "DM0": _sb(CH, F32), "tmp": _sb(5 * CH, F32),
    "thr": _sb(CH, F32), "wT": _sb(CH, F32), "far": _sb(CH, BF),
    "kp": _sb(CH, F16), "ysq": _sb(CH, F32), "yi": _sb(CH, I32), "yj": _sb(CH, I32),
    "offh": _sb(CH, U16), "offa": _sb(CH, U16), "offb": _sb(CH, U16), "offc": _sb(8, U16), "offt": _sb(8, U16),
    "DT": _sb(128, BF), "GH": _sb(1536, F16), "GL": _sb(1536, F16), "Drep": _sb(1536, BF),
    "xa": _sb(1536, BF), "xb": _sb(1536, BF), "aa": _sb(1536, BF), "bb": _sb(1536, BF),
    "cand": _sb(2 * CH, F32), "near": _sb(2 * CH, BF), "sel": _sb(2 * CH, F16), "rT": _sb(CH, F32), "rT2": _sb(CH, F32),
    "EQ": _sb(7 * CH, BF), "xq": _sb(CH, F32), "kk": _sb(CH, I32), "I4": _sb(128, BF),
    "Ds": _sb(RO * CH, BF), "ts": _sb(RO * CH, BF), "Dl": _sb(RO * CH, BF), "tl": _sb(RO * CH, BF), "nl": _sb(CH, BF),
    "tk": _sb(RO * CH, F32), "yts": _sb(RO * CH, F32), "ycs": _sb(CH, F32),
}
for _k in range(8):
    SCRATCH["b%d" % _k] = ("psum", [128, 512], F32)
SEMAPHORES = (["cv", "ca", "cp", "cg", "sent", "l_c0", "l_wt", "l_th", "l_hd", "l_xr", "l_nx", "s_yt", "s_yc"]
              + ["a%s%d" % (_x, _k) for _x in "DT" for _k in range(RO)])
_ORDER = {}


def depends(ops):
    by, last, dma, deps = {}, {}, 0.0, []
    for i, o in enumerate(ops):
        dep = set(o["after"])
        for (name, lo, hi, w) in o["acc"]:
            dep.update(j for (j, l2, h2, w2) in by.get(name, []) if (w or w2) and l2 < hi and lo < h2)
        for (name, lo, hi, w) in o["acc"]:
            if w:
                by[name] = [e for e in by.get(name, []) if not (lo <= e[1] and e[2] <= hi)]
            by.setdefault(name, []).append((i, lo, hi, w))
        for b in o["banks"]:
            if o["q"] == "p" and b in CHAINED:
                dep.update(last.get(b, ()))
                last[b] = (i,)
        dep.discard(i)
        deps.append(sorted(dep))
        if o["bytes"]:
            dma = max(dma, 1700.0) + o["bytes"] / CFG["bw"]
            o["lat"] = dma + 300.0
    return [(o["q"], o["lat"], o["busy"], o["banks"], [(j, 0.0 if o["q"] == "p" == ops[j]["q"] else CFG["wake"]) for j in d]
             + [(j, -ops[j]["lat"]) for j in ([o["order"]] if "order" in o else [])]) for o, d in zip(ops, deps)], CFG["wake"]


def place_calls(calls, wake, succ, prio):
    n = len(calls)
    left, start, done, eng, bank = [len(c[4]) for c in calls], [0.0] * n, [0.0] * n, {}, {}
    ready = [i for i in range(n) if not left[i]]
    while ready:
        i = max(ready, key=lambda k: prio[k])
        ready.remove(i)
        q, lat, busy, banks, dep = calls[i]
        t = 0.0
        for j, w in dep:
            if done[j] + w > t:
                t = done[j] + w
        if q != "x":
            iv, moved = eng.setdefault(q, []), True
            while moved:
                moved = False
                for (a, b) in iv:
                    if t < b and a < t + busy:
                        t, moved = b, True
                for bk in banks:
                    for (a, b, q2) in bank.get(bk, ()):
                        if t < b + wake and q2 != q and a < t + lat + wake:
                            t, moved = b + wake, True
            iv.append((t, t + busy))
            if len(iv) > 60:
                iv.sort()
                del iv[:20]
                iv[0] = (0.0, iv[0][1])
            for bk in banks:
                bank.setdefault(bk, []).append((t, t + lat, q))
        start[i], done[i] = t, t + lat
        for j in succ[i]:
            left[j] -= 1
            if not left[j]:
                ready.append(j)
    return sorted(range(n), key=lambda k: (start[k], k))


def span(calls, wake, order):
    free, done, bank = {}, [0.0] * len(calls), {}
    for i in order:
        q, lat, busy, banks, dep = calls[i]
        t = free.get(q, 0.0) if q != "x" else 0.0
        for j, w in dep:
            if done[j] + w > t:
                t = done[j] + w
        for b in banks:
            for q2, t2 in bank.setdefault(b, {}).items():
                if q2 != q and t2 + wake > t:
                    t = t2 + wake
        done[i], free[q] = t + lat, t + busy
        for b in banks:
            bank[b][q] = done[i]
    return max(done)


def schedule(make):
    base, sets = dict(CFG), []
    for m in base["vary"]:
        CFG.update(m)
        ops = make()
        sets.append(depends(ops))
        CFG.update(base)
    calls, wake = sets[0]
    n, succ, kinds, seen, r = len(calls), [[] for c in calls], {}, {}, [CFG["seed"]]
    for i, c in enumerate(calls):
        for j, w in c[4]:
            succ[j].append(i)
        seen[ops[i]["tag"]] = seen.get(ops[i]["tag"], 0) + 1
        kinds.setdefault((ops[i]["tag"][1], seen[ops[i]["tag"]]), []).append(i)
    keys = sorted(kinds, key=lambda k: kinds[k][0])

    def rnd():
        r[0] = (r[0] * 6364136223846793005 + 1442695040888963407) % 2 ** 64
        return (r[0] >> 11) / 2.0 ** 53

    def judge(p):
        order = place_calls(calls, wake, succ, p)
        return order, [span(c, w, order) for c, w in sets]

    prio = [-100.0 * i for i in range(n)]
    order, ref = judge(prio)
    cur, best, spans = 1.0, 1.0, ref
    for it in range(CFG["tries"]):
        p, d, run = list(prio), (rnd() + rnd() - 1) * (300, 800, 2500)[int(3 * rnd())], (1, 1, 1, 2, 4)[int(5 * rnd())]
        if rnd() < 0.3:
            x = int(n * rnd())
            for i in range(max(x, 6), min(n, x + run)):
                p[i] += d
        else:
            x = 6 + int((len(keys) - 6) * rnd())
            for k in keys[x:x + run]:
                for i in kinds[k]:
                    p[i] += d
        o2, v = judge(p)
        s = sum(a / b for a, b in zip(v, ref)) / len(ref)
        if s <= cur or rnd() < math.exp((cur - s) / (1e-6 + 0.0003 * (1 - it / CFG["tries"]))):
            cur, prio = s, p
            if s < best:
                best, order, spans = s, o2, v
    return order, spans


def build(g, core, T, topo, rank):
    n_ranks = len(T.cores)
    Q = {"a": g.scalar, "s": g.sync}
    ops, tag = [], [(-1, "setup")]
    cyc, fix = CFG["cyc"], CFG["fix"]

    def S(name, lo=0, hi=None, step=1, p1=128):
        t = T[name]
        if hi is None:
            hi = t.shape[1]
        ap = t[0:p1, lo:hi] if step == 1 else t[0:p1, lo:hi:step]
        return (ap, [(name, lo, hi)], (hi - lo + step - 1) // step, False)

    def IND(win, off):
        return (win[0].indirect(off[0]), win[1] + off[1], 16 * off[2], True)

    def op(q, issue, reads, writes, lat, busy=None, sem=None, inc=1, after=(), nbytes=0, own=True):
        acc = [r + (False,) for x in reads for r in x[1]] + [r + (True,) for x in writes for r in x[1]]
        ops.append({"q": q, "issue": issue, "acc": acc, "lat": lat, "busy": lat if busy is None else busy, "sem": sem or "c" + q,
                    "inc": inc, "after": after, "bytes": nbytes, "own": own, "tag": tag[0],
                    "banks": sorted(set(a[0] for a in acc if SCRATCH[a[0]][0] == "psum"))})
        return len(ops) - 1

    def cost(out, ins, mul=1.0):
        if ins[0][3]:
            return 55 + out[2] * CFG["gam"] * cyc
        if mul == 0.5 and any(SCRATCH[x[1][0][0]][2] in (F32, I32) for x in ins + [out]):
            mul = 1.0
        return fix + max(64, out[2] * mul) * cyc

    def col(x):
        return x[0] if isinstance(x, tuple) else x

    def ts(out, in0, s1, op0, s2=None, op1=None):
        ins = [x for x in (in0, s1, s2) if isinstance(x, tuple)]
        if op1 is None:
            op("v", lambda: g.vector.tensor_scalar(out[0], in0[0], col(s1), None, op0), ins, [out], cost(out, ins, 0.5))
        else:
            op("v", lambda: g.vector.tensor_scalar(out[0], in0[0], col(s1), col(s2), op0, op1), ins, [out], cost(out, ins, 0.5))

    def tt(out, a, b, o):
        both = SCRATCH[a[1][0][0]][0] == SCRATCH[b[1][0][0]][0]
        op("v", lambda: g.vector.tensor_tensor(out[0], a[0], b[0], o), [a, b], [out], cost(out, [a, b], 2.0 if both else 1.0))

    def cp(out, a):
        op("v", lambda: g.vector.tensor_copy(out[0], a[0]), [a], [out], cost(out, [a], 0.5))

    def scan(out, d0, d1, init, o0, o1):
        op("v", lambda: g.vector.tensor_tensor_scan(out[0], d0[0], d1[0], init, o0, o1), [d0, d1], [out], cost(out, [d0]))

    def fill(out, c):
        op("v", lambda: g.vector.memset(out[0], c), [], [out], cost(out, [out], 0.5))

    def act(out, a, f, bias=0.0, scale=1.0):
        ins = [x for x in (a, bias) if isinstance(x, tuple)]
        op("a", lambda: g.scalar.activation(out[0], a[0], f, bias=col(bias), scale=scale), ins, [out], cost(out, [a]))

    def mm(out, pairs, start=True, stop=True):
        def issue():
            for k, (l, r) in enumerate(pairs):
                ins = g.tensor.matmul(out[0], l[0], r[0], start and k == 0, stop and k == len(pairs) - 1)
            return ins
        c = sum(max(min(64, l[2]), r[2]) * (4 if SCRATCH[r[1][0][0]][2] == F32 else 1) for l, r in pairs) * CFG["pe"]
        op("p", issue, [x for pr in pairs for x in pr], [out], c)

    def iota(out, pattern, mult):
        if SCRATCH[out[1][0][0]][2] == I32:
            op("g", lambda: g.iota(out[0], pattern, 0, mult), [], [out], 130 + 2 * out[2] * cyc)
        else:
            op("g", lambda: g.iota(out[0], pattern, 0, mult, allow_small_or_imprecise_dtypes=True), [], [out], 130 + 2 * out[2] * cyc)

    def load(q, sem, out, src, nbytes):
        op(q, lambda: Q[q].dma_start(out[0], src), [], [out], 2000.0, 50.0, sem, 16, nbytes=nbytes)

    def move(src, dst, sem, t):
        to = T.cores[(rank + 1 + t % (n_ranks - 1)) % n_ranks]
        frm = T.cores[(rank - 1 - t % (n_ranks - 1)) % n_ranks]
        rid, pid = topo.addr(to, core)
        i = op("g", lambda: g.remote_dma(dst[0], src[0], T.sem[sem], T.sem["sent"], pid, rid, topo.mask(core, to)), [src], [],
               CFG["rissue"], None, "sent", len(topo.engines(core, to)), own=False)
        op("x", None, [], [dst], CFG["rem"] - CFG["rissue"], 0.0, sem, len(topo.engines(frm, core)), after=(i,), own=False)

    def places(out, sq, a, b):
        ts(a, sq, 1.0 / 32, ALU.mult, -8.40625, ALU.add)
        ts(b, a, HB - 1, ALU.bitwise_and)
        cp(out, b)

    load("s", "l_c0", S("c0s"), T.c0[:], 1)
    load("a", "l_wt", S("wts"), T.wt[:], 1)
    load("s", "l_hd", S("hds"), T.hd[:], 128 * HB * 4)
    load("a", "l_th", S("ths", 0, 1), T.th[:], 1)
    load("s", "l_nx", S("nxs", 0, V), T.nx[:], 128 * V * 4)
    load("s", "l_xr", S("xw", 0, V), T.xr[:], 128 * V * 2)

    iota(S("pi"), [[1, 16]], 1)
    iota(S("J"), [[1, 144]], 0)
    iota(S("Jg"), [[16, 8], [0, 16]], 0)
    iota(S("JE"), [[1, 32], [0, 16]], 0)
    iota(S("J16"), [[0, 6], [1, 16]], 0)
    i16, nx16, pv16 = S("ab", 0, 1), S("ab", 1, 2), S("ab", 15, 16)
    g16, pcol, J128 = S("cols", 0, 1), S("cols", 2, 3), S("J", 0, 128)
    ts(S("pa"), S("pi"), 15, ALU.bitwise_and)
    cp(S("ab"), S("pa"))
    tt(g16, S("pi", 0, 1), S("pa", 0, 1), ALU.subtract)
    ts(S("PT"), J128, g16, ALU.subtract, nx16, ALU.is_equal)
    ts(S("B"), S("Jg"), g16, ALU.is_equal)
    for k in range(8):
        mm(S("b7", 16 * k, 16 * k + 16), [(S("PT"), S("wts"))])
    tt(S("W"), S("b7", 0, 128), S("B"), ALU.mult)
    cp(pcol, S("pi", 0, 1))
    ts(S("N4"), J128, pcol, ALU.is_equal, -4096.0, ALU.mult)
    ts(S("PR"), J128, g16, ALU.subtract, pv16, ALU.is_equal)
    ts(S("I"), J128, pcol, ALU.is_equal)
    ts(S("dm"), S("J", 0, 16), i16, ALU.is_equal, -1.0, ALU.mult)

    def early():
        for d in range(16):
            ts(S("DG", 128 * d, 128 * d + 128), S("I"), S("dm", d, d + 1), ALU.mult)
        fill(S("xw", V, XW), FAR)
        fill(S("nxs", V, V + 8), V)
        ts(S("Z"), S("J"), g16, ALU.subtract, 15.0, ALU.is_equal)

    def by_u():
        iota(S("JU"), [[16, 256]], 0)
        ts(S("b16", 0, 1), i16, 16.0, ALU.add)
        act(S("usq"), S("JU"), AF.Square, bias=S("b16", 0, 1))
        places(S("offu"), S("usq"), S("ui"), S("uj"))
        cp(S("hdf"), S("hds"))
        w = 256 // CFG["cuts"]
        for k in range(CFG["cuts"]):
            act(S("hu", 16 * w * k, 16 * w * (k + 1)), IND(S("hdf"), S("offu", w * k, w * (k + 1))), AF.Identity)

    def late():
        act(S("NB"), S("B"), AF.Identity, scale=-1.0)
        act(S("IB"), S("I"), AF.Identity, scale=BIG)
        act(S("I32"), S("I"), AF.Identity)
        act(S("I4"), S("I"), AF.Identity, scale=0.25)
        cp(S("thf", 0, 1), S("ths", 0, 1))
        ts(S("Lt"), J128, pcol, ALU.is_gt)
        cp(S("B16"), S("B"))
        tt(S("Lu"), S("Lt"), S("B"), ALU.mult)
        tt(S("Lm"), S("I"), S("Lu"), ALU.subtract)
        ts(S("OD"), S("J16"), i16, ALU.not_equal, -BIG, ALU.mult)
        act(S("OD2"), S("OD"), AF.Identity, bias=-BIG)
        ts(S("RSB"), S("J16"), 0.0, ALU.not_equal, 2 * BIG, ALU.mult)
        ts(S("tmp", 0, CH), S("J", 0, CH), i16, ALU.add, -1.0, ALU.mult)
        tt(S("DM0"), S("tmp", 0, CH), S("RSB"), ALU.add)
        fill(S("tmp", CH, 2 * CH), 0.5)
        fill(S("tmp", 2 * CH, 3 * CH), 0.0)
        scan(S("thr"), S("tmp", CH, 2 * CH), S("tmp", 2 * CH, 3 * CH), 2.0, ALU.mult, ALU.add)
        ts(S("tmp", 3 * CH, 4 * CH), S("J16"), i16, ALU.is_equal, 0.5, ALU.mult)
        tt(S("tmp", 4 * CH, 5 * CH), S("tmp", 3 * CH, 4 * CH), S("thr"), ALU.mult)
        scan(S("wT"), S("RSB"), S("tmp", 4 * CH, 5 * CH), 0.0, ALU.min, ALU.max)
        fill(S("EQ"), 0.0)
        fill(S("far"), FAR)

    xwin = S("xw")
    place, used = {}, {}
    for name in sorted(CFG["bank"]):
        b = CFG["bank"][name]
        place[name] = used.get(b, 0)
        used[b] = place[name] + (128 if name == "DT" else CH)

    def P(name, c0=0, c1=CH, p1=128):
        return S(CFG["bank"][name], place[name] + c0, place[name] + c1, p1=p1)

    def big(name, c0, c1):
        return S(name, 16 * c0, 16 * c1)

    def rep(c0, c1, stop):
        j = c0 // 32
        lo, hi = 16 * (c0 - 32 * j), 16 * (c1 - 32 * j)
        R = S("b%d" % (2 + j), lo, hi)
        rows = slice(32 * j, 32 * j + 32)
        mm(R, [((T.DT[rows, 0:128], [("DT", 0, 128)], 128, False), (T.E32[rows, lo:hi], [("E32", lo, hi)], hi - lo, False))], stop=stop)
        return R

    def column_gather(c0, c1, q, off, xn, an):
        if q == "a":
            act(big(xn, c0, c1), IND(xwin, S(off, c0, c1)), AF.Identity, scale=-1.0)
            R = rep(c0, c1, False)
            mm(R, [(S("I"), big(xn, c0, c1))], start=False)
            act(big(an, c0, c1), R, AF.Abs)
        else:
            tt(big(xn, c0, c1), IND(xwin, S(off, c0, c1)), big("Drep", c0, c1), ALU.subtract)
            act(big(an, c0, c1), big(xn, c0, c1), AF.Abs)

    def rowsum(out, an, c0, c1):
        mm(out, [(S("Z", 15 - d, 143 - d), S(an, 16 * c0 + d, 16 * c1, 16)) for d in range(16)])

    def pieces(ws):
        return [(sum(ws[:k]), sum(ws[:k + 1])) for k in range(len(ws))]

    for t in range(RO):
        o, by = t * CH, t > 0 and CFG["byu"]
        tag[0] = (t, "round")
        C = [S("c0s")] if t == 0 else [S("Dl", o - CH, o), S("tl", o - CH, o)]
        Ds, xb = S("Ds", o, o + CH), CFG["xb"][min(t, 1)]
        xb = [p + (q,) for p, (w, q) in zip(pieces([w for w, q in xb]), xb)]
        xa = CFG["xa"][min(t, 1)]
        xa = [p + (q,) for p, (w, q) in zip(pieces([w for w, q in xa]), xa)]
        mm(P("s"), [(S("W"), c) for c in C])
        ts(S("kp"), P("s"), 2.0 ** -12, ALU.mult, 1535.5 + 2.0 ** -13, ALU.add)
        mm(P("u"), [(S("W"), c) for c in C] + [(S("N4"), S("kp"))])
        if by:
            ts(S("offh"), P("u"), 1536.0 * 4096, ALU.add)
        else:
            act(S("ysq"), P("u"), AF.Square, bias=1536.0 * 4096 + 16)
            places(S("offh"), S("ysq"), S("yi"), S("yj"))
        if t == 0:
            early()
            ts(S("pb", 0, 1), S("pi", 0, 1), 31, ALU.bitwise_and)
            cp(S("cols", 4, 5), S("pb", 0, 1))
            ts(S("E32"), S("JE"), S("cols", 4, 5), ALU.is_equal)
        mm(P("DT", 0, 128, p1=CH), [(c, S("PR")) for c in C])
        act(S("DT", 0, 128, p1=CH), P("DT", 0, 128, p1=CH), AF.Identity)
        mm(P("D"), [(S("PR"), c) for c in C])
        H, L = pieces(CFG["H"]), pieces(CFG["L"])
        steps = ([(p, "GH", S("hu") if by else S("hds"), "offh", "ca", "offa") for p in H]
                 + [(p, "GL", S("nxs"), "offa", "cb", "offb") for p in L])
        for k, (p, G, win, offi, reg, offo) in enumerate(steps):
            cp(big(G, *p), IND(win, S(offi, *p)))
            if k > 0:
                ts(S(steps[k - 1][5], *steps[k - 1][0]), P(steps[k - 1][4], *steps[k - 1][0]), -1.0, ALU.mult)
            mm(P(reg, *p), [(S("DG", 128 * d, 128 * d + 128), S(G, 16 * p[0] + d, 16 * p[1], 16)) for d in range(16)])
            if t == 0 and k == len(H) - 1 and CFG["byu"]:
                by_u()
        for j in range(3):
            ws = sorted(p for p in xa + xb if p[2] == "v" and p[0] // 32 == j)
            if ws:
                act(big("Drep", ws[0][0], max(p[1] for p in ws)), rep(ws[0][0], max(p[1] for p in ws), True), AF.Identity)
        act(Ds, P("D"), AF.Identity)
        move(Ds, S("Dl", o, o + CH), "aD%d" % t, t)
        for p in xa:
            column_gather(p[0], p[1], p[2], "offa", "xa", "aa")
        act(S("cand", 0, CH), P("ca"), AF.Identity)
        rowsum(P("da"), "aa", 0, CH)
        vs = [p for p in xb if p[2] == "v" and p[1] <= L[-1][0]][:1]
        for p in vs:
            column_gather(p[0], p[1], p[2], "offb", "xb", "bb")
        ts(S("offb", *L[-1]), P("cb", *L[-1]), -1.0, ALU.mult)
        for p in xb:
            if p not in vs:
                column_gather(p[0], p[1], p[2], "offb", "xb", "bb")
        act(S("cand", CH, 2 * CH), P("cb"), AF.Identity)
        if t == 0:
            late()
        m = CFG["sumb"]
        rowsum(P("db2", m, CH), "bb", m, CH)
        rowsum(P("db1", 0, m), "bb", 0, m)
        na, nb, sa, sb, th = S("near", 0, CH), S("near", CH, 2 * CH), S("sel", 0, CH), S("sel", CH, 2 * CH), S("thf", 0, 1)
        ts(na, P("da"), th, ALU.is_le, BIG, ALU.mult)
        mm(P("va"), [(S("I32"), S("cand", 0, CH)), (S("Lm"), na)])
        ts(sa, P("va"), V - BIG, ALU.add, 0.0, ALU.max)
        mm(P("vb"), [(S("I32"), S("cand", CH, 2 * CH)), (S("NB"), na)], stop=False)
        mm(P("M"), [(S("I"), S("OD")), (S("B16"), sa)], stop=False)
        mm(P("r"), [(S("B16"), sa)], stop=False)
        ts(S("near", CH + m, 2 * CH), P("db2", m, CH), th, ALU.is_le, BIG, ALU.mult)
        ts(S("near", CH, CH + m), P("db1", 0, m), th, ALU.is_le, BIG, ALU.mult)
        mm(P("vb"), [(S("Lm"), nb)], start=False)
        ts(sb, P("vb"), V - BIG, ALU.add, 0.0, ALU.max)
        mm(P("M"), [(S("B16"), sb)], start=False)
        mm(P("r"), [(S("B16"), sb)], start=False)
        scan(S("rT"), S("RSB"), P("M"), 0.0, ALU.min, ALU.max)
        offc = S("offc", 0, 6)
        ts(offc, S("rT", 15, CH, 16), -1.0, ALU.mult, float(V), ALU.add)
        act(S("xq"), IND(xwin, offc), AF.Identity, bias=-0.375, scale=0.25)
        mm(P("z"), [(S("I4"), Ds)])
        mm(P("cnt"), [(S("B"), na), (S("B"), nb)])
        act(S("EQ", 6 * CH, 7 * CH), P("cnt"), AF.Relu, bias=1.0, scale=-1.0)
        mm(P("S"), [(S("B"), S("EQ", 6 * CH, 7 * CH))], stop=False)
        for k in range(6):
            ts(S("EQ", k * CH + 16 * k, (k + 1) * CH), P("r", 16 * k, CH), S("rT", 16 * k + 15, 16 * k + 16), ALU.is_equal,
               S("wT", 16 * k + 15, 16 * k + 16), ALU.mult)
            if k:
                ops[-1]["order"] = len(ops) - 3
            mm(P("S"), [(S("B"), S("EQ", k * CH, (k + 1) * CH))], start=False, stop=k == 5)
        nl = S("nl")
        tt(S("kk"), S("xq"), P("z"), ALU.subtract)
        tt(P("kb"), P("S"), S("thr"), ALU.is_lt)
        tt(S("ts", o, o + CH), S("kk"), P("kb"), ALU.mult)
        move(S("ts", o, o + CH), S("tl", o, o + CH), "aT%d" % t, t)
        tag[0] = (t, "after")
        tt(nl, P("S"), S("thr"), ALU.is_lt)
        both = [(S("B16"), sa), (S("B16"), sb), (S("IB"), nl)]
        mm(P("Y"), both)
        act(S("tk", o, o + CH), P("Y"), AF.Relu, bias=-BIG)
        if t < RO - 1:
            mm(P("M2"), [(S("I"), S("OD2"))] + both)
            scan(S("rT2"), S("DM0"), P("M2"), 0.0, ALU.min, ALU.max)
            ts(S("offt", 0, 6), S("rT2", 15, CH, 16), -1.0, ALU.mult, float(V), ALU.add)
            ind = IND(xwin, S("offt", 0, 6))
            op("v", lambda ind=ind: g.vector.tensor_copy(ind[0], T.far[:]), [S("far"), S("offt", 0, 6)], [xwin], 50 + 3 * CH * cyc)

    tag[0] = (RO, "out")
    o = (RO - 1) * CH
    tt(S("ycs"), S("Dl", o, o + CH), S("tl", o, o + CH), ALU.add)
    op("s", lambda: g.sync.dma_start(T.yc[:], T.ycs[:]), [S("ycs")], [], 2000.0, 50.0, "s_yc", 16)
    act(S("yts"), S("tk"), AF.Identity, bias=float(V), scale=-1.0)
    op("a", lambda: g.scalar.dma_start(T.yt[:], T.yts[0:128:16, :]), [S("yts")], [], 2000.0, 50.0, "s_yt", 16)
    return ops


def rank_program(g, core, T, topo):
    rank = T.rank_of(core)
    if rank is None:
        return
    if "order" not in _ORDER:
        _ORDER["order"], _ORDER["span"] = schedule(lambda: build(g, core, T, topo, rank))
    ops = build(g, core, T, topo, rank)
    Q = {"v": g.vector, "a": g.scalar, "p": g.tensor, "g": g, "s": g.sync}
    count, waited, hist = {}, {}, {}
    known = {q: {} for q in Q}

    def wait(q, sem, n):
        Q[q].wait_ge(T.sem[sem], n)
        known[q][sem] = n
        waited[sem] = max(waited.get(sem, 0), n)

    for i in _ORDER["order"]:
        o = ops[i]
        q, sem, need = o["q"], o["sem"], {}
        if q != "x":
            for (name, lo, hi, wr) in o["acc"]:
                bank = SCRATCH[name][0] == "psum"
                for (l2, h2, w2, q2, tok, clock) in hist.get(name, []):
                    if q2 == q == "p":
                        continue
                    if (((wr or w2) and l2 < hi and lo < h2) or (bank and q2 != q)) and need.get(tok[0], (0, None))[0] < tok[1]:
                        need[tok[0]] = (tok[1], clock)
            todo = [(s, n, c) for s, (n, c) in need.items() if known[q].get(s, 0) < n]
            for s, n, c in [(s, n, c) for (s, n, c) in todo if not any(s2 != s and c2.get(s, 0) >= n for (s2, n2, c2) in todo)]:
                wait(q, s, n)
                for s2, n2 in c.items():
                    known[q][s2] = max(known[q].get(s2, 0), n2)
        count[sem] = count.get(sem, 0) + o["inc"]
        if o["issue"] is not None:
            ins = o["issue"]()
            if o["own"]:
                ins.then_inc(T.sem[sem], o["inc"])
        tok, clock = (sem, count[sem]), dict(known.get(q, {}))
        for (name, lo, hi, wr) in o["acc"]:
            old = [e for e in hist.get(name, []) if not (e[3] == q and e[4][0] == sem and e[0] == lo and e[1] == hi and e[2] == wr)]
            hist[name] = old + [(lo, hi, wr, q, tok, clock)]
    for sem in SEMAPHORES:
        if waited.get(sem, 0) < count.get(sem, 0):
            wait("g", sem, count[sem])
